import numpy as np
import ml_dtypes


def mxq(x, axis, fmt="e4m3"):
    dtype, down = {"e4m3": (ml_dtypes.float8_e4m3fn, 7), "e5m2": (ml_dtypes.float8_e5m2, 14)}[fmt]
    v = np.moveaxis(np.asarray(x, np.float32).astype(ml_dtypes.bfloat16).astype(np.float64), axis, -1)
    blocks = v.reshape(v.shape[:-1] + (-1, 32))
    amax = np.abs(blocks).max(-1, keepdims=True)
    byte = np.maximum(np.where(amax > 0, np.frexp(amax)[1] - 1 + 127, 0) - down, 1)
    scale = np.exp2(byte - 127.0)
    codes = (blocks / scale).astype(np.float32).astype(dtype).astype(np.float64)
    return np.moveaxis((codes * scale).reshape(v.shape), -1, axis)


WIDE = False


def mx_kscale(k):
    if not WIDE:
        return np.ones(k)
    levels = np.array([10, -10, 5, -5, 0])
    if k % 512:
        return np.exp2(np.random.permutation(np.resize(levels, k // 32))).repeat(32)
    a = np.empty((k // 512, 16))
    for p in range(k // 512):
        a[p, :8] = np.random.permutation(np.resize(levels, 8))
        for g in range(8):
            far = levels[np.abs(levels - a[p, g]) >= 10]
            a[p, g + 8] = far[np.random.randint(len(far))]
    return np.exp2(a.ravel()).repeat(32)


BF16 = ml_dtypes.bfloat16


def bf(x):
    return np.asarray(x, np.float32).astype(BF16)


def f64(x):
    return np.asarray(x).astype(np.float64)


B, S, R, D, E, T = 2, 1024, 1024, 512, 512, 2


def draw0():
    s, t = mx_kscale(S), mx_kscale(D)
    return {
        "x": bf(np.random.standard_normal((B, S, D)) * s[:, None]),
        "mp": bf(np.random.standard_normal((R, S)) / np.sqrt(S) / s[None, :]),
        "mq": bf(np.random.standard_normal((R, S)) / np.sqrt(S) / s[None, :]),
        "mr": bf(np.random.standard_normal((R, S)) / np.sqrt(S) / s[None, :]),
        "coef": bf(np.random.uniform(0.4, 1.0, (T, D))),
        "gain": bf((1.0 + 0.1 * np.random.standard_normal(D)) * t),
        "wo": bf(np.random.standard_normal((D, E)) / np.sqrt(D) / t[:, None]),
    }


def mix_time(m, xq):
    return mxq(f64(m), 1, "e4m3") @ xq


def core(x, mp, mq, mr, coef, gain, wo):
    c = f64(coef)
    xq = mxq(f64(x), 1, "e4m3")
    p = mix_time(mp, xq)
    q = mix_time(mq, xq)
    r = mix_time(mr, xq)
    h = c[0] + c[1] * r
    y = p * (1.0 + q * h)
    z = y * f64(gain)
    return mxq(z, 2, "e4m3") @ mxq(f64(wo), 0, "e4m3")


def e4m3fn_bytes(y):
    return np.clip(np.asarray(y, np.float64), -448.0, 448.0).astype(np.float32).astype(ml_dtypes.float8_e4m3fn).view(np.uint8)


def e4m3fn_values(b):
    return np.asarray(b, np.uint8).view(ml_dtypes.float8_e4m3fn).astype(np.float64)


def setup_inputs():
    d = draw0()
    x0 = np.asarray(d['x']).astype(np.float64)
    s = (np.max(np.abs(x0), axis=(0, 2), keepdims=True) / 448.0).astype(np.float32)
    out = {}
    for k, v in d.items():
        if k == 'x':
            out['x_bytes'] = e4m3fn_bytes(x0 / s.astype(np.float64))
            out['x_scale'] = s
        else:
            out[k] = v
    return out


def reference(x_bytes, x_scale, mp, mq, mr, coef, gain, wo):
    return core(e4m3fn_values(x_bytes) * x_scale.astype(np.float64), mp, mq, mr, coef, gain, wo)

@@ -1,0 +1,335 @@
+from contextlib import ExitStack
+
+import concourse.mybir as mybir
+from concourse.masks import make_identity
+
+B, S, R, D, E = 2, 1024, 1024, 512, 512
+FLOPS = 2 * B * R * D * (3 * S + E)
+
+F32 = mybir.dt.float32
+BF16 = mybir.dt.bfloat16
+U32 = mybir.dt.uint32
+U8 = mybir.dt.uint8
+FP8 = mybir.dt.float8_e4m3fn
+FP8X4 = mybir.dt.float8_e4m3fn_x4
+ALU = mybir.AluOpType
+ACT = mybir.ActivationFunctionType
+
+P = 128
+PACK = 4
+NG = S // (P * PACK)
+TB = 256
+NA = TB // P
+NTB = R // TB
+NJ = D // P
+ORDER = ((0, 0), (0, 1), (0, 2), (0, 3), (1, 0), (1, 1), (1, 2), (1, 3))
+
+
+def tile_volterrathirdordermixer_kernel(tc, x_bytes, x_scale, mp, mq, mr, coef, gain, wo, out):
+    nc = tc.nc
+    mats = (mr, mq, mp)
+    with ExitStack() as ctx:
+        keep = ctx.enter_context(tc.tile_pool(name="keep", bufs=1))
+        work = ctx.enter_context(tc.tile_pool(name="work", bufs=2))
+        accs = ctx.enter_context(tc.psum_pool(name="accs", bufs=5))
+        misc = ctx.enter_context(tc.psum_pool(name="misc", bufs=3))
+        ctx.enter_context(tc.manual_schedule())
+
+        xs = keep.tile([P, NG, PACK], F32, name="xs")
+        nc.scalar.dma_start(out=xs[:], in_=x_scale.rearrange("o (g p t) u -> p g (o t u)", p=P, t=PACK))
+        cf = keep.tile([P, 2, NJ], BF16, name="cf")
+        nc.gpsimd.dma_start(out=cf[:], in_=coef.rearrange("c (p j) -> p c j", j=NJ))
+        gn = keep.tile([P, NJ], BF16, name="gn")
+        nc.gpsimd.dma_start(out=gn[:], in_=gain.rearrange("(p j) -> p j", j=NJ))
+
+        xraw = {}
+        mraw = {}
+
+        def load_x(b, gs=range(NG)):
+            for g in gs:
+                t = keep.tile([P, PACK, D], U8, name="xraw%d%d" % (b, g))
+                nc.sync.dma_start(
+                    out=t[:], in_=x_bytes[b].rearrange("(g p t) d -> g p t d", p=P, t=PACK)[g]
+                )
+                xraw[b, g] = t
+
+        def load_m(tb, mats_i=range(3)):
+            for i in mats_i:
+                t = keep.tile([P, NA, S], BF16, name="mraw%d%d" % (i, tb))
+                nc.sync.dma_start(
+                    out=t[:], in_=mats[i][tb * TB : (tb + 1) * TB, :].rearrange("(p a) k -> p a k", a=NA)
+                )
+                mraw[i, tb] = t
+
+        load_x(0)
+        load_m(0)
+        load_m(1)
+        load_x(1)
+        load_m(2, (0,))
+        woraw = keep.tile([P, PACK, E], BF16, name="woraw")
+        nc.sync.dma_start(out=woraw[:], in_=wo.rearrange("(p j) e -> p j e", j=PACK))
+        load_m(2, (1, 2))
+        load_m(3)
+
+        dummy = keep.tile([P, 1], F32, name="dummy")
+        nc.gpsimd.memset(dummy[:], 0.0)
+        ident = keep.tile([P, P], F32, name="ident")
+        make_identity(nc, ident[:])
+        nc.scalar.activation(out=dummy[:], in_=dummy[:], func=ACT.Identity)
+        hs = keep.tile([P, NJ], F32, name="hs")
+        hb = keep.tile([P, NJ], F32, name="hb")
+        gf = keep.tile([P, NJ], F32, name="gf")
+        nc.gpsimd.tensor_tensor(out=hs[:], in0=cf[:, 1, :], in1=gn[:], op=ALU.mult)
+        nc.gpsimd.tensor_tensor(out=hb[:], in0=cf[:, 0, :], in1=gn[:], op=ALU.mult)
+        nc.gpsimd.tensor_copy(out=gf[:], in_=gn[:])
+
+        xwide, xgrp, xcode, xsc = {}, {}, {}, {}
+
+        def x_widen(b, g, t, on_vector):
+            if t == 0:
+                xwide[b, g] = work.tile([P, PACK, D], BF16, name="xwide", bufs=4)
+            dst = xwide[b, g][:, t, :]
+            src = xraw[b, g][:, t, :].bitcast(FP8)
+            sc = xs[:, g, t : t + 1]
+            if on_vector:
+                nc.vector.tensor_scalar(out=dst, in0=src, scalar1=sc, scalar2=None, op0=ALU.mult)
+            else:
+                nc.scalar.activation(out=dst, in_=src, func=ACT.Copy, scale=sc)
+
+        def x_group(b, g, j0=0, j1=NJ, eng=None):
+            if j0 == 0:
+                xgrp[b, g] = work.tile([P, D * PACK], BF16, name="xgrp", align_bytes=64)
+            (eng or nc.vector.tensor_copy)(
+                out=xgrp[b, g][:].rearrange("p (j m t) -> p j m t", j=NJ, t=PACK)[:, j0:j1],
+                in_=xwide[b, g][:].rearrange("p t (m j) -> p j m t", j=NJ)[:, j0:j1],
+            )
+
+        def x_quant(b, g):
+            xcode[b, g] = keep.tile([P, D], U32, name="xcode%d%d" % (b, g), align_bytes=64)
+            xsc[b, g] = keep.tile([P, D], U8, name="xsc%d%d" % (b, g), align_bytes=64)
+            nc.vector.quantize_mx(out=xcode[b, g][:].bitcast(FP8X4), scales=xsc[b, g][:], in_=xgrp[b, g][:])
+
+        wogrp = keep.tile([P, E * PACK], BF16, name="wogrp", align_bytes=64)
+        wocode = keep.tile([P, E], U32, name="wocode", align_bytes=64)
+        wosc = keep.tile([P, E], U8, name="wosc", align_bytes=64)
+
+        def wo_group():
+            nc.vector.tensor_copy(
+                out=wogrp[:].rearrange("p (e j) -> p e j", j=PACK), in_=woraw[:].rearrange("p j e -> p e j")
+            )
+
+        def wo_quant():
+            nc.vector.quantize_mx(out=wocode[:].bitcast(FP8X4), scales=wosc[:], in_=wogrp[:])
+
+        mT, mcode, msc, tp = {}, {}, {}, {}
+
+        def m_transpose(i, tb):
+            words = mraw[i, tb][:].rearrange("p a k -> p (a k)").bitcast(F32)
+            for a in range(NA):
+                t = misc.tile([P, NG, 2, P], F32, name="bank")
+                for g in range(NG):
+                    for u in range(2):
+                        w0 = a * (S // 2) + g * 256 + u
+                        nc.tensor.transpose(t[:, g, u, :], words[:, w0 : w0 + 255 : 2], ident[:])
+                tp[i, tb, a] = t
+
+        def m_evac(i, tb):
+            mT[i, tb] = work.tile([P, NG * TB * PACK], BF16, name="mT", align_bytes=64, bufs=7)
+            dst = mT[i, tb][:].bitcast(F32).rearrange("p (g t u) -> p g t u", g=NG, u=2)
+            for a in range(NA):
+                nc.scalar.copy(
+                    out=dst[:, :, a * P : (a + 1) * P, :], in_=tp[i, tb, a][:].rearrange("p g u r -> p g r u")
+                )
+
+        def m_quant(i, tb):
+            mcode[i, tb] = keep.tile([P, NG * TB], U32, name="mcode%d%d" % (i, tb), align_bytes=64)
+            msc[i, tb] = keep.tile([P, NG * TB], U8, name="msc%d%d" % (i, tb), align_bytes=64)
+            nc.vector.quantize_mx(
+                out=mcode[i, tb][:].bitcast(FP8X4), scales=msc[i, tb][:], in_=mT[i, tb][:]
+            )
+
+        acc, hh, uu, zp, zg, zcode, zsc, ores = {}, {}, {}, {}, {}, {}, {}, {}
+
+        def mix(n, h, i):
+            b, tb = ORDER[n]
+            t = accs.tile([P, 2, TB], F32, name="acc")
+            for jj in range(2):
+                cols = slice((2 * h + jj) * P, (2 * h + jj + 1) * P)
+                for g in range(NG):
+                    rows = slice(g * TB, (g + 1) * TB)
+                    nc.tensor.matmul_mx(
+                        out=t[:, jj, :],
+                        lhsT=xcode[b, g][:, cols].bitcast(FP8X4),
+                        lhsT_scale=xsc[b, g][:, cols],
+                        rhs=mcode[i, tb][:, rows].bitcast(FP8X4),
+                        rhs_scale=msc[i, tb][:, rows],
+                        start=(g == 0),
+                        stop=(g == NG - 1),
+                    )
+            acc[n, h, i] = t
+
+        def h_part(n, h):
+            hh[n, h] = work.tile([P, 2, TB], F32, name="hh", bufs=3)
+            for jj in range(2):
+                j = 2 * h + jj
+                nc.scalar.activation(
+                    out=hh[n, h][:, jj, :],
+                    in_=acc[n, h, 0][:, jj, :],
+                    func=ACT.Identity,
+                    scale=hs[:, j : j + 1],
+                    bias=hb[:, j : j + 1],
+                )
+
+        def u_part(n, h):
+            uu[n, h] = work.tile([P, 2, TB], F32, name="uu")
+            nc.vector.tensor_tensor(out=uu[n, h][:], in0=acc[n, h, 1][:], in1=hh[n, h][:], op=ALU.mult)
+
+        def z_part(n, h):
+            if h == 0:
+                zp[n] = work.tile([P, NJ, TB], BF16, name="zp")
+            for jj in range(2):
+                j = 2 * h + jj
+                nc.vector.scalar_tensor_tensor(
+                    out=zp[n][:, j, :],
+                    in0=uu[n, h][:, jj, :],
+                    scalar=gf[:, j : j + 1],
+                    in1=acc[n, h, 2][:, jj, :],
+                    op0=ALU.add,
+                    op1=ALU.mult,
+                )
+
+        def z_group(n, t0, t1):
+            if t0 == 0:
+                zg[n] = work.tile([P, TB * PACK], BF16, name="zg", align_bytes=64)
+            nc.vector.tensor_copy(
+                out=zg[n][:].rearrange("p (t j) -> p t j", j=PACK)[:, t0:t1, :],
+                in_=zp[n][:, :, t0:t1].rearrange("p j t -> p t j"),
+            )
+
+        def z_quant(n, t0, t1):
+            if t0 == 0:
+                zcode[n] = work.tile([P, TB], U32, name="zcode", align_bytes=64, bufs=3)
+                zsc[n] = work.tile([P, TB], U8, name="zsc", align_bytes=64, bufs=3)
+            nc.vector.quantize_mx(
+                out=zcode[n][:, t0:t1].bitcast(FP8X4),
+                scales=zsc[n][:, t0:t1],
+                in_=zg[n][:, t0 * PACK : t1 * PACK],
+            )
+
+        def project(n, a):
+            t = misc.tile([P, E], F32, name="bank")
+            cols = slice(a * P, (a + 1) * P)
+            nc.tensor.matmul_mx(
+                out=t[:],
+                lhsT=zcode[n][:, cols].bitcast(FP8X4),
+                lhsT_scale=zsc[n][:, cols],
+                rhs=wocode[:].bitcast(FP8X4),
+                rhs_scale=wosc[:],
+                start=True,
+                stop=True,
+            )
+            tp[n, a] = t
+
+        def o_evac(n, a, on_vector):
+            if a == 0:
+                ores[n] = work.tile([P, NA, E], F32, name="ores", bufs=3)
+            if on_vector:
+                nc.vector.tensor_copy(out=ores[n][:, a, :], in_=tp[n, a][:])
+            else:
+                nc.scalar.copy(out=ores[n][:, a, :], in_=tp[n, a][:])
+
+        def o_view(n):
+            b, tb = ORDER[n]
+            return out[b, tb * TB : (tb + 1) * TB, :].rearrange("(p a) e -> p a e", a=NA)
+
+        def o_store(n):
+            nc.sync.dma_start(out=o_view(n), in_=ores[n][:])
+
+        for t in range(PACK):
+            x_widen(0, 0, t, True)
+        x_group(0, 0)
+        for t in range(PACK):
+            x_widen(0, 1, t, t % 2 == 0)
+        x_group(0, 1)
+        x_quant(0, 0)
+        x_quant(0, 1)
+        for i in range(3):
+            m_transpose(i, 0)
+            m_evac(i, 0)
+        for i in range(3):
+            m_quant(i, 0)
+        for i in range(3):
+            m_transpose(i, 1)
+            m_evac(i, 1)
+        for t in range(PACK):
+            x_widen(1, 0, t, True)
+        turns = {(0, 1): (0, 2), (0, 3): (1, 2), (1, 1): (2, 2), (1, 3): (0, 3), (2, 1): (1, 3), (2, 3): (2, 3)}
+        vq = {
+            (0, 0): (lambda: m_quant(0, 1),),
+            (0, 2): (lambda: m_quant(1, 1), lambda: x_group(1, 0)),
+            (0, 4): (lambda: m_quant(2, 1), wo_group),
+            (0, 5): (lambda: m_quant(0, 2), wo_quant),
+            (1, 1): (lambda: m_quant(1, 2),),
+            (1, 3): (lambda: m_quant(2, 2),),
+            (1, 4): (lambda: x_quant(1, 0),),
+            (2, 1): (lambda: m_quant(0, 3),),
+            (2, 4): (lambda: m_quant(1, 3),),
+            (2, 2): (lambda: x_group(1, 1, 0, 2, nc.scalar.copy),),
+            (2, 5): (lambda: m_quant(2, 3), lambda: x_group(1, 1, 2, 4, nc.scalar.copy),),
+            (3, 4): (lambda: x_quant(1, 1),),
+        }
+        widen_at = {(0, 0): (4,), (1, 0): (5,), (1, 2): (6,), (1, 4): (7,)}
+        units = B * NTB
+
+        def side(n, s):
+            if (n, s) in turns:
+                m_transpose(*turns[n, s])
+                m_evac(*turns[n, s])
+            for w in widen_at.get((n, s), ()):
+                x_widen(1, w // PACK, w % PACK, False)
+            for f in vq.get((n, s), ()):
+                f()
+
+        for n in range(units):
+            mix(n, 0, 0)
+            h_part(n, 0)
+            if n > 1:
+                for a in range(NA):
+                    o_evac(n - 2, a, False)
+                o_store(n - 2)
+            side(n, 0)
+            if n > 0:
+                z_group(n - 1, 0, TB)
+            mix(n, 0, 1)
+            u_part(n, 0)
+            if n > 0:
+                z_quant(n - 1, 0, TB)
+            side(n, 1)
+            mix(n, 0, 2)
+            z_part(n, 0)
+            side(n, 2)
+            mix(n, 1, 0)
+            h_part(n, 1)
+            side(n, 3)
+            mix(n, 1, 1)
+            u_part(n, 1)
+            side(n, 4)
+            mix(n, 1, 2)
+            z_part(n, 1)
+            side(n, 5)
+            if n > 0:
+                for a in range(NA):
+                    project(n - 1, a)
+
+        last = units - 1
+        for a in range(NA):
+            o_evac(last - 1, a, False)
+        o_store(last - 1)
+        for a in range(NA):
+            z_group(last, a * P, (a + 1) * P)
+        for a in range(NA):
+            z_quant(last, a * P, (a + 1) * P)
+        for a in range(NA):
+            project(last, a)
+            o_evac(last, a, a == 1)
+            nc.sync.dma_start(out=o_view(last)[:, a, :], in_=ores[last][:, a, :])

@@ -42,6 +42,9 @@ def tile_volterrathirdordermixer_kernel(tc, x_bytes, x_scale, mp, mq, mr, coef, 
         gn = keep.tile([P, NJ], BF16, name="gn")
         nc.gpsimd.dma_start(out=gn[:], in_=gain.rearrange("(p j) -> p j", j=NJ))
 
+        zeros = keep.tile([P, 512], BF16, name="zeros")
+        nc.vector.memset(zeros[:], 0.0)
+
         xraw = {}
         mraw = {}
 
@@ -120,6 +123,11 @@ def tile_volterrathirdordermixer_kernel(tc, x_bytes, x_scale, mp, mq, mr, coef, 
 
         def wo_quant():
             nc.vector.quantize_mx(out=wocode[:].bitcast(FP8X4), scales=wosc[:], in_=wogrp[:])
+
+        def warm(k):
+            t = misc.tile([P, 512], F32, name="bank")
+            for i in range(k):
+                nc.tensor.matmul(t[:], lhsT=zeros[:, 0:P], rhs=zeros[:], start=True, stop=True)
 
         mT, mcode, msc, tp = {}, {}, {}, {}
 
@@ -253,17 +261,17 @@ def tile_volterrathirdordermixer_kernel(tc, x_bytes, x_scale, mp, mq, mr, coef, 
         x_group(0, 1)
         x_quant(0, 0)
         x_quant(0, 1)
+        warm(9)
         for i in range(3):
             m_transpose(i, 0)
             m_evac(i, 0)
+            warm((2, 2, 2)[i])
         for i in range(3):
             m_quant(i, 0)
-        for i in range(3):
-            m_transpose(i, 1)
-            m_evac(i, 1)
+
         for t in range(PACK):
             x_widen(1, 0, t, True)
-        turns = {(0, 1): (0, 2), (0, 3): (1, 2), (1, 1): (2, 2), (1, 3): (0, 3), (2, 1): (1, 3), (2, 3): (2, 3)}
+        turns = {(0, 0): (0, 1), (0, 2): (1, 1), (0, 4): (2, 1), (0, 5): (0, 2), (1, 1): (1, 2), (1, 3): (2, 2), (1, 5): (0, 3), (2, 1): (1, 3), (2, 3): (2, 3)}
         vq = {
             (0, 0): (lambda: m_quant(0, 1),),
             (0, 2): (lambda: m_quant(1, 1), lambda: x_group(1, 0)),

@@ -31,8 +31,8 @@ def tile_volterrathirdordermixer_kernel(tc, x_bytes, x_scale, mp, mq, mr, coef, 
     with ExitStack() as ctx:
         keep = ctx.enter_context(tc.tile_pool(name="keep", bufs=1))
         work = ctx.enter_context(tc.tile_pool(name="work", bufs=2))
-        accs = ctx.enter_context(tc.psum_pool(name="accs", bufs=5))
-        misc = ctx.enter_context(tc.psum_pool(name="misc", bufs=3))
+        accs = ctx.enter_context(tc.psum_pool(name="accs", bufs=4))
+        misc = ctx.enter_context(tc.psum_pool(name="misc", bufs=4))
         ctx.enter_context(tc.manual_schedule())
 
         xs = keep.tile([P, NG, PACK], F32, name="xs")
@@ -100,7 +100,7 @@ def tile_volterrathirdordermixer_kernel(tc, x_bytes, x_scale, mp, mq, mr, coef, 
                 nc.scalar.activation(out=dst, in_=src, func=ACT.Copy, scale=sc)
 
         def x_group(b, g, j0=0, j1=NJ, eng=None):
-            if j0 == 0:
+            if (b, g) not in xgrp:
                 xgrp[b, g] = work.tile([P, D * PACK], BF16, name="xgrp", align_bytes=64)
             (eng or nc.vector.tensor_copy)(
                 out=xgrp[b, g][:].rearrange("p (j m t) -> p j m t", j=NJ, t=PACK)[:, j0:j1],
@@ -125,15 +125,17 @@ def tile_volterrathirdordermixer_kernel(tc, x_bytes, x_scale, mp, mq, mr, coef, 
             nc.vector.quantize_mx(out=wocode[:].bitcast(FP8X4), scales=wosc[:], in_=wogrp[:])
 
         def warm(k):
-            t = misc.tile([P, 512], F32, name="bank")
+            if k == 0:
+                return
+            t = accs.tile([P, 512], F32, name="acc")
             for i in range(k):
                 nc.tensor.matmul(t[:], lhsT=zeros[:, 0:P], rhs=zeros[:], start=True, stop=True)
 
         mT, mcode, msc, tp = {}, {}, {}, {}
 
-        def m_transpose(i, tb):
+        def m_transpose(i, tb, blocks=range(NA)):
             words = mraw[i, tb][:].rearrange("p a k -> p (a k)").bitcast(F32)
-            for a in range(NA):
+            for a in blocks:
                 t = misc.tile([P, NG, 2, P], F32, name="bank")
                 for g in range(NG):
                     for u in range(2):
@@ -141,10 +143,11 @@ def tile_volterrathirdordermixer_kernel(tc, x_bytes, x_scale, mp, mq, mr, coef, 
                         nc.tensor.transpose(t[:, g, u, :], words[:, w0 : w0 + 255 : 2], ident[:])
                 tp[i, tb, a] = t
 
-        def m_evac(i, tb):
-            mT[i, tb] = work.tile([P, NG * TB * PACK], BF16, name="mT", align_bytes=64, bufs=7)
+        def m_evac(i, tb, blocks=range(NA)):
+            if 0 in blocks:
+                mT[i, tb] = work.tile([P, NG * TB * PACK], BF16, name="mT", align_bytes=64, bufs=7)
             dst = mT[i, tb][:].bitcast(F32).rearrange("p (g t u) -> p g t u", g=NG, u=2)
-            for a in range(NA):
+            for a in blocks:
                 nc.scalar.copy(
                     out=dst[:, :, a * P : (a + 1) * P, :], in_=tp[i, tb, a][:].rearrange("p g u r -> p g r u")
                 )
@@ -192,24 +195,24 @@ def tile_volterrathirdordermixer_kernel(tc, x_bytes, x_scale, mp, mq, mr, coef, 
             uu[n, h] = work.tile([P, 2, TB], F32, name="uu")
             nc.vector.tensor_tensor(out=uu[n, h][:], in0=acc[n, h, 1][:], in1=hh[n, h][:], op=ALU.mult)
 
-        def z_part(n, h):
+        def z_part(n, h, t0=0, t1=TB):
             if h == 0:
                 zp[n] = work.tile([P, NJ, TB], BF16, name="zp")
             for jj in range(2):
                 j = 2 * h + jj
                 nc.vector.scalar_tensor_tensor(
-                    out=zp[n][:, j, :],
-                    in0=uu[n, h][:, jj, :],
+                    out=zp[n][:, j, t0:t1],
+                    in0=uu[n, h][:, jj, t0:t1],
                     scalar=gf[:, j : j + 1],
-                    in1=acc[n, h, 2][:, jj, :],
+                    in1=acc[n, h, 2][:, jj, t0:t1],
                     op0=ALU.add,
                     op1=ALU.mult,
                 )
 
-        def z_group(n, t0, t1):
+        def z_group(n, t0, t1, eng=None):
             if t0 == 0:
                 zg[n] = work.tile([P, TB * PACK], BF16, name="zg", align_bytes=64)
-            nc.vector.tensor_copy(
+            (eng or nc.vector.tensor_copy)(
                 out=zg[n][:].rearrange("p (t j) -> p t j", j=PACK)[:, t0:t1, :],
                 in_=zp[n][:, :, t0:t1].rearrange("p j t -> p t j"),
             )
@@ -224,27 +227,27 @@ def tile_volterrathirdordermixer_kernel(tc, x_bytes, x_scale, mp, mq, mr, coef, 
                 in_=zg[n][:, t0 * PACK : t1 * PACK],
             )
 
-        def project(n, a):
-            t = misc.tile([P, E], F32, name="bank")
+        def project(n, a, e0=0, e1=E):
+            t = misc.tile([P, e1 - e0], F32, name="bank")
             cols = slice(a * P, (a + 1) * P)
             nc.tensor.matmul_mx(
                 out=t[:],
                 lhsT=zcode[n][:, cols].bitcast(FP8X4),
                 lhsT_scale=zsc[n][:, cols],
-                rhs=wocode[:].bitcast(FP8X4),
-                rhs_scale=wosc[:],
+                rhs=wocode[:, e0:e1].bitcast(FP8X4),
+                rhs_scale=wosc[:, e0:e1],
                 start=True,
                 stop=True,
             )
-            tp[n, a] = t
+            tp[n, a, e0] = t
 
-        def o_evac(n, a, on_vector):
-            if a == 0:
+        def o_evac(n, a, on_vector, e0=0, e1=E):
+            if a == 0 and e0 == 0:
                 ores[n] = work.tile([P, NA, E], F32, name="ores", bufs=3)
             if on_vector:
-                nc.vector.tensor_copy(out=ores[n][:, a, :], in_=tp[n, a][:])
+                nc.vector.tensor_copy(out=ores[n][:, a, e0:e1], in_=tp[n, a, e0][:])
             else:
-                nc.scalar.copy(out=ores[n][:, a, :], in_=tp[n, a][:])
+                nc.scalar.copy(out=ores[n][:, a, e0:e1], in_=tp[n, a, e0][:])
 
         def o_view(n):
             b, tb = ORDER[n]
@@ -255,44 +258,48 @@ def tile_volterrathirdordermixer_kernel(tc, x_bytes, x_scale, mp, mq, mr, coef, 
 
         for t in range(PACK):
             x_widen(0, 0, t, True)
-        x_group(0, 0)
         for t in range(PACK):
             x_widen(0, 1, t, t % 2 == 0)
-        x_group(0, 1)
+        x_group(0, 0)
+        x_group(0, 1, 2, 4, nc.scalar.copy)
+        x_group(0, 1, 0, 2)
         x_quant(0, 0)
         x_quant(0, 1)
-        warm(9)
+        warm(16)
         for i in range(3):
-            m_transpose(i, 0)
-            m_evac(i, 0)
-            warm((2, 2, 2)[i])
+            for a in range(NA):
+                m_transpose(i, 0, (a,))
+                m_evac(i, 0, (a,))
+                warm((0, 2, 0, 2, 0, 0)[NA * i + a])
         for i in range(3):
             m_quant(i, 0)
 
         for t in range(PACK):
             x_widen(1, 0, t, True)
-        turns = {(0, 0): (0, 1), (0, 2): (1, 1), (0, 4): (2, 1), (0, 5): (0, 2), (1, 1): (1, 2), (1, 3): (2, 2), (1, 5): (0, 3), (2, 1): (1, 3), (2, 3): (2, 3)}
+        turns = {(0, 0): ((0, 1),), (0, 2): ((1, 1),), (0, 4): ((2, 1),), (1, 0): ((0, 2),), (1, 2): ((1, 2),), (1, 4): ((2, 2),), (2, 0): ((0, 3),), (2, 2): ((1, 3),), (2, 4): ((2, 3),)}
         vq = {
-            (0, 0): (lambda: m_quant(0, 1),),
-            (0, 2): (lambda: m_quant(1, 1), lambda: x_group(1, 0)),
-            (0, 4): (lambda: m_quant(2, 1), wo_group),
-            (0, 5): (lambda: m_quant(0, 2), wo_quant),
-            (1, 1): (lambda: m_quant(1, 2),),
-            (1, 3): (lambda: m_quant(2, 2),),
-            (1, 4): (lambda: x_quant(1, 0),),
-            (2, 1): (lambda: m_quant(0, 3),),
-            (2, 4): (lambda: m_quant(1, 3),),
-            (2, 2): (lambda: x_group(1, 1, 0, 2, nc.scalar.copy),),
-            (2, 5): (lambda: m_quant(2, 3), lambda: x_group(1, 1, 2, 4, nc.scalar.copy),),
-            (3, 4): (lambda: x_quant(1, 1),),
+            (0, 1): (lambda: m_quant(0, 1),),
+            (0, 2): (lambda: x_group(1, 0),),
+            (0, 3): (lambda: m_quant(1, 1),),
+            (0, 4): (wo_group,),
+            (0, 5): (lambda: m_quant(2, 1),),
+            (1, 0): (wo_quant,),
+            (1, 1): (lambda: m_quant(0, 2),),
+            (1, 2): (lambda: x_quant(1, 0),),
+            (1, 3): (lambda: m_quant(1, 2),),
+            (1, 5): (lambda: m_quant(2, 2), lambda: x_group(1, 1, 0, 2, nc.scalar.copy)),
+            (2, 1): (lambda: m_quant(0, 3), lambda: x_group(1, 1, 2, 4, nc.scalar.copy)),
+            (2, 3): (lambda: m_quant(1, 3), lambda: x_quant(1, 1)),
+            (2, 5): (lambda: m_quant(2, 3),),
         }
-        widen_at = {(0, 0): (4,), (1, 0): (5,), (1, 2): (6,), (1, 4): (7,)}
+        widen_at = {(0, 1): (4,), (0, 5): (5,), (1, 1): (6,), (1, 3): (7,)}
         units = B * NTB
 
         def side(n, s):
-            if (n, s) in turns:
-                m_transpose(*turns[n, s])
-                m_evac(*turns[n, s])
+            for blk in turns.get((n, s), ()):
+                m_transpose(*blk)
+            for blk in turns.get((n, s), ()):
+                m_evac(*blk)
             for w in widen_at.get((n, s), ()):
                 x_widen(1, w // PACK, w % PACK, False)
             for f in vq.get((n, s), ()):
@@ -307,7 +314,7 @@ def tile_volterrathirdordermixer_kernel(tc, x_bytes, x_scale, mp, mq, mr, coef, 
                 o_store(n - 2)
             side(n, 0)
             if n > 0:
-                z_group(n - 1, 0, TB)
+                z_group(n - 1, 0, TB, nc.scalar.copy if n - 1 in () else None)
             mix(n, 0, 1)
             u_part(n, 0)
             if n > 0:
@@ -323,7 +330,8 @@ def tile_volterrathirdordermixer_kernel(tc, x_bytes, x_scale, mp, mq, mr, coef, 
             u_part(n, 1)
             side(n, 4)
             mix(n, 1, 2)
-            z_part(n, 1)
+            if n + 1 < units:
+                z_part(n, 1)
             side(n, 5)
             if n > 0:
                 for a in range(NA):
@@ -331,13 +339,19 @@ def tile_volterrathirdordermixer_kernel(tc, x_bytes, x_scale, mp, mq, mr, coef, 
 
         last = units - 1
         for a in range(NA):
+            z_part(last, 1, a * P, (a + 1) * P)
+        for a in range(NA):
             o_evac(last - 1, a, False)
         o_store(last - 1)
-        for a in range(NA):
-            z_group(last, a * P, (a + 1) * P)
-        for a in range(NA):
-            z_quant(last, a * P, (a + 1) * P)
-        for a in range(NA):
-            project(last, a)
-            o_evac(last, a, a == 1)
-            nc.sync.dma_start(out=o_view(last)[:, a, :], in_=ores[last][:, a, :])
+        z_group(last, 0, P)
+        z_group(last, P, TB)
+        z_quant(last, 0, P)
+        z_quant(last, P, TB)
+        project(last, 0)
+        project(last, 1, 0, E // 2)
+        project(last, 1, E // 2, E)
+        o_evac(last, 0, False)
+        nc.sync.dma_start(out=o_view(last)[:, 0, :], in_=ores[last][:, 0, :])
+        o_evac(last, 1, True, 0, E // 2)
+        o_evac(last, 1, True, E // 2, E)
+        nc.sync.dma_start(out=o_view(last)[:, 1, :], in_=ores[last][:, 1, :])

@@ -103,14 +103,19 @@ def tile_volterrathirdordermixer_kernel(tc, x_bytes, x_scale, mp, mq, mr, coef, 
             if (b, g) not in xgrp:
                 xgrp[b, g] = work.tile([P, D * PACK], BF16, name="xgrp", align_bytes=64)
             (eng or nc.vector.tensor_copy)(
-                out=xgrp[b, g][:].rearrange("p (j m t) -> p j m t", j=NJ, t=PACK)[:, j0:j1],
-                in_=xwide[b, g][:].rearrange("p t (m j) -> p j m t", j=NJ)[:, j0:j1],
+                out=xgrp[b, g][:].rearrange("p (j q i t) -> p q j i t", j=NJ, i=2, t=PACK)[:, 16 * j0 : 16 * j1],
+                in_=xwide[b, g][:].rearrange("p t (q i j) -> p q j i t", j=NJ, i=2)[:, 16 * j0 : 16 * j1],
             )
 
-        def x_quant(b, g):
-            xcode[b, g] = keep.tile([P, D], U32, name="xcode%d%d" % (b, g), align_bytes=64)
-            xsc[b, g] = keep.tile([P, D], U8, name="xsc%d%d" % (b, g), align_bytes=64)
-            nc.vector.quantize_mx(out=xcode[b, g][:].bitcast(FP8X4), scales=xsc[b, g][:], in_=xgrp[b, g][:])
+        def x_quant(b, g, j0=0, j1=NJ):
+            if (b, g) not in xcode:
+                xcode[b, g] = keep.tile([P, D], U32, name="xcode%d%d" % (b, g), align_bytes=64)
+                xsc[b, g] = keep.tile([P, D], U8, name="xsc%d%d" % (b, g), align_bytes=64)
+            nc.vector.quantize_mx(
+                out=xcode[b, g][:, j0 * P : j1 * P].bitcast(FP8X4),
+                scales=xsc[b, g][:, j0 * P : j1 * P],
+                in_=xgrp[b, g][:, j0 * P * PACK : j1 * P * PACK],
+            )
 
         wogrp = keep.tile([P, E * PACK], BF16, name="wogrp", align_bytes=64)
         wocode = keep.tile([P, E], U32, name="wocode", align_bytes=64)
@@ -219,8 +224,8 @@ def tile_volterrathirdordermixer_kernel(tc, x_bytes, x_scale, mp, mq, mr, coef, 
 
         def z_quant(n, t0, t1):
             if t0 == 0:
-                zcode[n] = work.tile([P, TB], U32, name="zcode", align_bytes=64, bufs=3)
-                zsc[n] = work.tile([P, TB], U8, name="zsc", align_bytes=64, bufs=3)
+                zcode[n] = work.tile([P, TB], U32, name="zcode", align_bytes=64, bufs=4)
+                zsc[n] = work.tile([P, TB], U8, name="zsc", align_bytes=64, bufs=4)
             nc.vector.quantize_mx(
                 out=zcode[n][:, t0:t1].bitcast(FP8X4),
                 scales=zsc[n][:, t0:t1],
@@ -265,7 +270,7 @@ def tile_volterrathirdordermixer_kernel(tc, x_bytes, x_scale, mp, mq, mr, coef, 
         x_group(0, 1, 0, 2)
         x_quant(0, 0)
         x_quant(0, 1)
-        warm(16)
+        warm(13)
         for i in range(3):
             for a in range(NA):
                 m_transpose(i, 0, (a,))
@@ -274,75 +279,94 @@ def tile_volterrathirdordermixer_kernel(tc, x_bytes, x_scale, mp, mq, mr, coef, 
         for i in range(3):
             m_quant(i, 0)
 
-        for t in range(PACK):
-            x_widen(1, 0, t, True)
-        turns = {(0, 0): ((0, 1),), (0, 2): ((1, 1),), (0, 4): ((2, 1),), (1, 0): ((0, 2),), (1, 2): ((1, 2),), (1, 4): ((2, 2),), (2, 0): ((0, 3),), (2, 2): ((1, 3),), (2, 4): ((2, 3),)}
-        vq = {
-            (0, 1): (lambda: m_quant(0, 1),),
-            (0, 2): (lambda: x_group(1, 0),),
-            (0, 3): (lambda: m_quant(1, 1),),
-            (0, 4): (wo_group,),
-            (0, 5): (lambda: m_quant(2, 1),),
-            (1, 0): (wo_quant,),
-            (1, 1): (lambda: m_quant(0, 2),),
-            (1, 2): (lambda: x_quant(1, 0),),
-            (1, 3): (lambda: m_quant(1, 2),),
-            (1, 5): (lambda: m_quant(2, 2), lambda: x_group(1, 1, 0, 2, nc.scalar.copy)),
-            (2, 1): (lambda: m_quant(0, 3), lambda: x_group(1, 1, 2, 4, nc.scalar.copy)),
-            (2, 3): (lambda: m_quant(1, 3), lambda: x_quant(1, 1)),
-            (2, 5): (lambda: m_quant(2, 3),),
+        beside = {
+            (0, -1): (('widen', 0, True), ('widen', 2, True), ('widen', 3, False),),
+            (0, 0): (('turn', 0, 1), ('widen', 1, True), ('widen', 4, False),),
+            (0, 1): (('mq', 0, 1), ('turn', 1, 1), ('wog',),),
+            (0, 2): (('mq', 1, 1),),
+            (0, 3): (('turn', 2, 1), ('widen', 6, False), ('mq', 2, 1), ('widen', 5, False),),
+            (0, 4): (('group', 0, 0, 4, False),),
+            (0, 5): (('zg', 0, False), ('widen', 7, False),),
+            (1, 0): (('turn', 0, 2), ('woq',),),
+            (1, 1): (('turn', 1, 2), ('zq', 0),),
+            (1, 2): (('group', 1, 0, 2, True), ('mq', 0, 2),),
+            (1, 3): (('turn', 1, 3),),
+            (1, 4): (('mq', 1, 2), ('turn', 2, 2),),
+            (1, 5): (('proj', 0),),
+            (2, 0): (('oev', 0, False), ('mq', 2, 2), ('mq', 1, 3),),
+            (2, 1): (('turn', 0, 3), ('zg', 1, False), ('xq', 0),),
+            (2, 2): (('mq', 0, 3), ('group', 1, 2, 4, True),),
+            (2, 3): (('xq', 1),),
+            (2, 4): (('zq', 1), ('turn', 2, 3),),
+            (3, 0): (('zg', 2, True), ('mq', 2, 3),),
+            (3, 1): (('proj', 1),),
+            (3, 2): (('zq', 2),),
+            (3, 5): (('zg', 3, False),),
+            (4, 1): (('proj', 2), ('zq', 3),),
+            (4, 2): (('oev', 1, False),),
+            (4, 4): (('oev', 2, False),),
+            (4, 5): (('proj', 3),),
+            (5, 0): (('zg', 4, False),),
+            (5, 1): (('zq', 4),),
+            (5, 4): (('oev', 3, False),),
+            (5, 5): (('zg', 5, False), ('proj', 4),),
+            (6, 1): (('zq', 5), ('oev', 4, False),),
+            (7, 0): (('zg', 6, False),),
+            (7, 1): (('zq', 6),),
+            (7, 4): (('proj', 5), ('oev', 5, False),),
+            (7, 5): (('proj', 6),),
+            (7, 6): (('oev', 6, False),),
         }
-        widen_at = {(0, 1): (4,), (0, 5): (5,), (1, 1): (6,), (1, 3): (7,)}
         units = B * NTB
 
         def side(n, s):
-            for blk in turns.get((n, s), ()):
-                m_transpose(*blk)
-            for blk in turns.get((n, s), ()):
-                m_evac(*blk)
-            for w in widen_at.get((n, s), ()):
-                x_widen(1, w // PACK, w % PACK, False)
-            for f in vq.get((n, s), ()):
-                f()
+            for op in beside.get((n, s), ()):
+                kind, args = op[0], op[1:]
+                if kind == "turn":
+                    m_transpose(*args)
+                    m_evac(*args)
+                elif kind == "mq":
+                    m_quant(*args)
+                elif kind == "widen":
+                    x_widen(1, args[0] // PACK, args[0] % PACK, args[1])
+                elif kind == "group":
+                    x_group(1, args[0], args[1], args[2], nc.scalar.copy if args[3] else None)
+                elif kind == "xq":
+                    x_quant(1, args[0])
+                elif kind == "wog":
+                    wo_group()
+                elif kind == "woq":
+                    wo_quant()
+                elif kind == "zg":
+                    z_group(args[0], 0, TB, nc.scalar.copy if args[1] else None)
+                elif kind == "zq":
+                    z_quant(args[0], 0, TB)
+                elif kind == "proj":
+                    for a in range(NA):
+                        project(args[0], a)
+                elif kind == "oev":
+                    for a in range(NA):
+                        o_evac(args[0], a, args[1])
+                    o_store(args[0])
 
+        side(0, -1)
         for n in range(units):
-            mix(n, 0, 0)
-            h_part(n, 0)
-            if n > 1:
-                for a in range(NA):
-                    o_evac(n - 2, a, False)
-                o_store(n - 2)
-            side(n, 0)
-            if n > 0:
-                z_group(n - 1, 0, TB, nc.scalar.copy if n - 1 in () else None)
-            mix(n, 0, 1)
-            u_part(n, 0)
-            if n > 0:
-                z_quant(n - 1, 0, TB)
-            side(n, 1)
-            mix(n, 0, 2)
-            z_part(n, 0)
-            side(n, 2)
-            mix(n, 1, 0)
-            h_part(n, 1)
-            side(n, 3)
-            mix(n, 1, 1)
-            u_part(n, 1)
-            side(n, 4)
-            mix(n, 1, 2)
-            if n + 1 < units:
-                z_part(n, 1)
-            side(n, 5)
-            if n > 0:
-                for a in range(NA):
-                    project(n - 1, a)
+            for h in range(2):
+                mix(n, h, 0)
+                h_part(n, h)
+                side(n, 3 * h)
+                mix(n, h, 1)
+                u_part(n, h)
+                side(n, 3 * h + 1)
+                mix(n, h, 2)
+                if (n, h) != (units - 1, 1):
+                    z_part(n, h)
+                side(n, 3 * h + 2)
 
         last = units - 1
         for a in range(NA):
             z_part(last, 1, a * P, (a + 1) * P)
-        for a in range(NA):
-            o_evac(last - 1, a, False)
-        o_store(last - 1)
+        side(last, 6)
         z_group(last, 0, P)
         z_group(last, P, TB)
         z_quant(last, 0, P)

from contextlib import ExitStack

import concourse.mybir as mybir
from concourse.masks import make_identity

B, S, R, D, E = 2, 1024, 1024, 512, 512
FLOPS = 2 * B * R * D * (3 * S + E)

F32 = mybir.dt.float32
BF16 = mybir.dt.bfloat16
U32 = mybir.dt.uint32
U8 = mybir.dt.uint8
FP8 = mybir.dt.float8_e4m3fn
FP8X4 = mybir.dt.float8_e4m3fn_x4
ALU = mybir.AluOpType
ACT = mybir.ActivationFunctionType

P = 128
PACK = 4
NG = S // (P * PACK)
TB = 256
NA = TB // P
NTB = R // TB
NJ = D // P
ORDER = ((0, 0), (0, 1), (0, 2), (0, 3), (1, 0), (1, 1), (1, 2), (1, 3))


def tile_volterrathirdordermixer_kernel(tc, x_bytes, x_scale, mp, mq, mr, coef, gain, wo, out):
    nc = tc.nc
    mats = (mr, mq, mp)
    with ExitStack() as ctx:
        keep = ctx.enter_context(tc.tile_pool(name="keep", bufs=1))
        work = ctx.enter_context(tc.tile_pool(name="work", bufs=2))
        accs = ctx.enter_context(tc.psum_pool(name="accs", bufs=4))
        misc = ctx.enter_context(tc.psum_pool(name="misc", bufs=4))
        ctx.enter_context(tc.manual_schedule())

        xs = keep.tile([P, NG, PACK], F32, name="xs")
        nc.scalar.dma_start(out=xs[:], in_=x_scale.rearrange("o (g p t) u -> p g (o t u)", p=P, t=PACK))
        cf = keep.tile([P, 2, NJ], BF16, name="cf")
        nc.gpsimd.dma_start(out=cf[:], in_=coef.rearrange("c (p j) -> p c j", j=NJ))
        gn = keep.tile([P, NJ], BF16, name="gn")
        nc.gpsimd.dma_start(out=gn[:], in_=gain.rearrange("(p j) -> p j", j=NJ))

        zeros = keep.tile([P, 512], BF16, name="zeros")
        nc.vector.memset(zeros[:], 0.0)

        xraw = {}
        mraw = {}

        def load_x(b, gs=range(NG)):
            for g in gs:
                t = keep.tile([P, PACK, D], U8, name="xraw%d%d" % (b, g))
                nc.sync.dma_start(
                    out=t[:], in_=x_bytes[b].rearrange("(g p t) d -> g p t d", p=P, t=PACK)[g]
                )
                xraw[b, g] = t

        def load_m(tb, mats_i=range(3)):
            for i in mats_i:
                t = keep.tile([P, NA, S], BF16, name="mraw%d%d" % (i, tb))
                nc.sync.dma_start(
                    out=t[:], in_=mats[i][tb * TB : (tb + 1) * TB, :].rearrange("(p a) k -> p a k", a=NA)
                )
                mraw[i, tb] = t

        load_x(0)
        load_m(0)
        load_m(1)
        load_x(1)
        load_m(2, (0,))
        woraw = keep.tile([P, PACK, E], BF16, name="woraw")
        nc.sync.dma_start(out=woraw[:], in_=wo.rearrange("(p j) e -> p j e", j=PACK))
        load_m(2, (1, 2))
        load_m(3)

        dummy = keep.tile([P, 1], F32, name="dummy")
        nc.gpsimd.memset(dummy[:], 0.0)
        ident = keep.tile([P, P], F32, name="ident")
        make_identity(nc, ident[:])
        nc.scalar.activation(out=dummy[:], in_=dummy[:], func=ACT.Identity)
        hs = keep.tile([P, NJ], F32, name="hs")
        hb = keep.tile([P, NJ], F32, name="hb")
        gf = keep.tile([P, NJ], F32, name="gf")
        nc.gpsimd.tensor_tensor(out=hs[:], in0=cf[:, 1, :], in1=gn[:], op=ALU.mult)
        nc.gpsimd.tensor_tensor(out=hb[:], in0=cf[:, 0, :], in1=gn[:], op=ALU.mult)
        nc.gpsimd.tensor_copy(out=gf[:], in_=gn[:])

        xwide, xgrp, xcode, xsc = {}, {}, {}, {}

        def x_widen(b, g, t, on_vector):
            if t == 0:
                xwide[b, g] = work.tile([P, PACK, D], BF16, name="xwide", bufs=4)
            dst = xwide[b, g][:, t, :]
            src = xraw[b, g][:, t, :].bitcast(FP8)
            sc = xs[:, g, t : t + 1]
            if on_vector:
                nc.vector.tensor_scalar(out=dst, in0=src, scalar1=sc, scalar2=None, op0=ALU.mult)
            else:
                nc.scalar.activation(out=dst, in_=src, func=ACT.Copy, scale=sc)

        def x_group(b, g, j0=0, j1=NJ, eng=None):
            if (b, g) not in xgrp:
                xgrp[b, g] = work.tile([P, D * PACK], BF16, name="xgrp", align_bytes=64)
            (eng or nc.vector.tensor_copy)(
                out=xgrp[b, g][:].rearrange("p (j q i t) -> p q j i t", j=NJ, i=2, t=PACK)[:, 16 * j0 : 16 * j1],
                in_=xwide[b, g][:].rearrange("p t (q i j) -> p q j i t", j=NJ, i=2)[:, 16 * j0 : 16 * j1],
            )

        def x_quant(b, g, j0=0, j1=NJ):
            if (b, g) not in xcode:
                xcode[b, g] = keep.tile([P, D], U32, name="xcode%d%d" % (b, g), align_bytes=64)
                xsc[b, g] = keep.tile([P, D], U8, name="xsc%d%d" % (b, g), align_bytes=64)
            nc.vector.quantize_mx(
                out=xcode[b, g][:, j0 * P : j1 * P].bitcast(FP8X4),
                scales=xsc[b, g][:, j0 * P : j1 * P],
                in_=xgrp[b, g][:, j0 * P * PACK : j1 * P * PACK],
            )

        wogrp = keep.tile([P, E * PACK], BF16, name="wogrp", align_bytes=64)
        wocode = keep.tile([P, E], U32, name="wocode", align_bytes=64)
        wosc = keep.tile([P, E], U8, name="wosc", align_bytes=64)

        def wo_group():
            nc.vector.tensor_copy(
                out=wogrp[:].rearrange("p (e j) -> p e j", j=PACK), in_=woraw[:].rearrange("p j e -> p e j")
            )

        def wo_quant():
            nc.vector.quantize_mx(out=wocode[:].bitcast(FP8X4), scales=wosc[:], in_=wogrp[:])

        def warm(k):
            if k == 0:
                return
            t = accs.tile([P, 512], F32, name="acc")
            for i in range(k):
                nc.tensor.matmul(t[:], lhsT=zeros[:, 0:P], rhs=zeros[:], start=True, stop=True)

        mT, mcode, msc, tp = {}, {}, {}, {}

        def m_transpose(i, tb, blocks=range(NA)):
            words = mraw[i, tb][:].rearrange("p a k -> p (a k)").bitcast(F32)
            for a in blocks:
                t = misc.tile([P, NG, 2, P], F32, name="bank")
                for g in range(NG):
                    for u in range(2):
                        w0 = a * (S // 2) + g * 256 + u
                        nc.tensor.transpose(t[:, g, u, :], words[:, w0 : w0 + 255 : 2], ident[:])
                tp[i, tb, a] = t

        def m_evac(i, tb, blocks=range(NA)):
            if 0 in blocks:
                mT[i, tb] = work.tile([P, NG * TB * PACK], BF16, name="mT", align_bytes=64, bufs=7)
            dst = mT[i, tb][:].bitcast(F32).rearrange("p (g t u) -> p g t u", g=NG, u=2)
            for a in blocks:
                nc.scalar.copy(
                    out=dst[:, :, a * P : (a + 1) * P, :], in_=tp[i, tb, a][:].rearrange("p g u r -> p g r u")
                )

        def m_quant(i, tb):
            mcode[i, tb] = keep.tile([P, NG * TB], U32, name="mcode%d%d" % (i, tb), align_bytes=64)
            msc[i, tb] = keep.tile([P, NG * TB], U8, name="msc%d%d" % (i, tb), align_bytes=64)
            nc.vector.quantize_mx(
                out=mcode[i, tb][:].bitcast(FP8X4), scales=msc[i, tb][:], in_=mT[i, tb][:]
            )

        acc, hh, uu, zp, zg, zcode, zsc, ores = {}, {}, {}, {}, {}, {}, {}, {}

        def mix(n, h, i):
            b, tb = ORDER[n]
            t = accs.tile([P, 2, TB], F32, name="acc")
            for jj in range(2):
                cols = slice((2 * h + jj) * P, (2 * h + jj + 1) * P)
                for g in range(NG):
                    rows = slice(g * TB, (g + 1) * TB)
                    nc.tensor.matmul_mx(
                        out=t[:, jj, :],
                        lhsT=xcode[b, g][:, cols].bitcast(FP8X4),
                        lhsT_scale=xsc[b, g][:, cols],
                        rhs=mcode[i, tb][:, rows].bitcast(FP8X4),
                        rhs_scale=msc[i, tb][:, rows],
                        start=(g == 0),
                        stop=(g == NG - 1),
                    )
            acc[n, h, i] = t

        def h_part(n, h):
            hh[n, h] = work.tile([P, 2, TB], F32, name="hh", bufs=3)
            for jj in range(2):
                j = 2 * h + jj
                nc.scalar.activation(
                    out=hh[n, h][:, jj, :],
                    in_=acc[n, h, 0][:, jj, :],
                    func=ACT.Identity,
                    scale=hs[:, j : j + 1],
                    bias=hb[:, j : j + 1],
                )

        def u_part(n, h):
            uu[n, h] = work.tile([P, 2, TB], F32, name="uu")
            nc.vector.tensor_tensor(out=uu[n, h][:], in0=acc[n, h, 1][:], in1=hh[n, h][:], op=ALU.mult)

        def z_part(n, h, t0=0, t1=TB):
            if h == 0:
                zp[n] = work.tile([P, NJ, TB], BF16, name="zp")
            for jj in range(2):
                j = 2 * h + jj
                nc.vector.scalar_tensor_tensor(
                    out=zp[n][:, j, t0:t1],
                    in0=uu[n, h][:, jj, t0:t1],
                    scalar=gf[:, j : j + 1],
                    in1=acc[n, h, 2][:, jj, t0:t1],
                    op0=ALU.add,
                    op1=ALU.mult,
                )

        def z_group(n, t0, t1, eng=None):
            if t0 == 0:
                zg[n] = work.tile([P, TB * PACK], BF16, name="zg", align_bytes=64)
            (eng or nc.vector.tensor_copy)(
                out=zg[n][:].rearrange("p (t j) -> p t j", j=PACK)[:, t0:t1, :],
                in_=zp[n][:, :, t0:t1].rearrange("p j t -> p t j"),
            )

        def z_quant(n, t0, t1):
            if t0 == 0:
                zcode[n] = work.tile([P, TB], U32, name="zcode", align_bytes=64, bufs=4)
                zsc[n] = work.tile([P, TB], U8, name="zsc", align_bytes=64, bufs=4)
            nc.vector.quantize_mx(
                out=zcode[n][:, t0:t1].bitcast(FP8X4),
                scales=zsc[n][:, t0:t1],
                in_=zg[n][:, t0 * PACK : t1 * PACK],
            )

        def project(n, a, e0=0, e1=E):
            t = misc.tile([P, e1 - e0], F32, name="bank")
            cols = slice(a * P, (a + 1) * P)
            nc.tensor.matmul_mx(
                out=t[:],
                lhsT=zcode[n][:, cols].bitcast(FP8X4),
                lhsT_scale=zsc[n][:, cols],
                rhs=wocode[:, e0:e1].bitcast(FP8X4),
                rhs_scale=wosc[:, e0:e1],
                start=True,
                stop=True,
            )
            tp[n, a, e0] = t

        def o_evac(n, a, on_vector, e0=0, e1=E):
            if a == 0 and e0 == 0:
                ores[n] = work.tile([P, NA, E], F32, name="ores", bufs=3)
            if on_vector:
                nc.vector.tensor_copy(out=ores[n][:, a, e0:e1], in_=tp[n, a, e0][:])
            else:
                nc.scalar.copy(out=ores[n][:, a, e0:e1], in_=tp[n, a, e0][:])

        def o_view(n):
            b, tb = ORDER[n]
            return out[b, tb * TB : (tb + 1) * TB, :].rearrange("(p a) e -> p a e", a=NA)

        def o_store(n):
            nc.sync.dma_start(out=o_view(n), in_=ores[n][:])

        for t in range(PACK):
            x_widen(0, 0, t, True)
        for t in range(PACK):
            x_widen(0, 1, t, t % 2 == 0)
        x_group(0, 0)
        x_group(0, 1, 2, 4, nc.scalar.copy)
        x_group(0, 1, 0, 2)
        x_quant(0, 0)
        x_quant(0, 1)
        warm(13)
        for i in range(3):
            for a in range(NA):
                m_transpose(i, 0, (a,))
                m_evac(i, 0, (a,))
                warm((0, 2, 0, 2, 0, 0)[NA * i + a])
        for i in range(3):
            m_quant(i, 0)

        beside = {
            (0, -1): (('widen', 0, True), ('widen', 2, True), ('widen', 3, False),),
            (0, 0): (('turn', 0, 1), ('widen', 1, True), ('widen', 4, False),),
            (0, 1): (('mq', 0, 1), ('turn', 1, 1), ('wog',),),
            (0, 2): (('mq', 1, 1),),
            (0, 3): (('turn', 2, 1), ('widen', 6, False), ('mq', 2, 1), ('widen', 5, False),),
            (0, 4): (('group', 0, 0, 4, False),),
            (0, 5): (('zg', 0, False), ('widen', 7, False),),
            (1, 0): (('turn', 0, 2), ('woq',),),
            (1, 1): (('turn', 1, 2), ('zq', 0),),
            (1, 2): (('group', 1, 0, 2, True), ('mq', 0, 2),),
            (1, 3): (('turn', 1, 3),),
            (1, 4): (('mq', 1, 2), ('turn', 2, 2),),
            (1, 5): (('proj', 0),),
            (2, 0): (('oev', 0, False), ('mq', 2, 2), ('mq', 1, 3),),
            (2, 1): (('turn', 0, 3), ('zg', 1, False), ('xq', 0),),
            (2, 2): (('mq', 0, 3), ('group', 1, 2, 4, True),),
            (2, 3): (('xq', 1),),
            (2, 4): (('zq', 1), ('turn', 2, 3),),
            (3, 0): (('zg', 2, True), ('mq', 2, 3),),
            (3, 1): (('proj', 1),),
            (3, 2): (('zq', 2),),
            (3, 5): (('zg', 3, False),),
            (4, 1): (('proj', 2), ('zq', 3),),
            (4, 2): (('oev', 1, False),),
            (4, 4): (('oev', 2, False),),
            (4, 5): (('proj', 3),),
            (5, 0): (('zg', 4, False),),
            (5, 1): (('zq', 4),),
            (5, 4): (('oev', 3, False),),
            (5, 5): (('zg', 5, False), ('proj', 4),),
            (6, 1): (('zq', 5), ('oev', 4, False),),
            (7, 0): (('zg', 6, False),),
            (7, 1): (('zq', 6),),
            (7, 4): (('proj', 5), ('oev', 5, False),),
            (7, 5): (('proj', 6),),
            (7, 6): (('oev', 6, False),),
        }
        units = B * NTB

        def side(n, s):
            for op in beside.get((n, s), ()):
                kind, args = op[0], op[1:]
                if kind == "turn":
                    m_transpose(*args)
                    m_evac(*args)
                elif kind == "mq":
                    m_quant(*args)
                elif kind == "widen":
                    x_widen(1, args[0] // PACK, args[0] % PACK, args[1])
                elif kind == "group":
                    x_group(1, args[0], args[1], args[2], nc.scalar.copy if args[3] else None)
                elif kind == "xq":
                    x_quant(1, args[0])
                elif kind == "wog":
                    wo_group()
                elif kind == "woq":
                    wo_quant()
                elif kind == "zg":
                    z_group(args[0], 0, TB, nc.scalar.copy if args[1] else None)
                elif kind == "zq":
                    z_quant(args[0], 0, TB)
                elif kind == "proj":
                    for a in range(NA):
                        project(args[0], a)
                elif kind == "oev":
                    for a in range(NA):
                        o_evac(args[0], a, args[1])
                    o_store(args[0])

        side(0, -1)
        for n in range(units):
            for h in range(2):
                mix(n, h, 0)
                h_part(n, h)
                side(n, 3 * h)
                mix(n, h, 1)
                u_part(n, h)
                side(n, 3 * h + 1)
                mix(n, h, 2)
                if (n, h) != (units - 1, 1):
                    z_part(n, h)
                side(n, 3 * h + 2)

        last = units - 1
        for a in range(NA):
            z_part(last, 1, a * P, (a + 1) * P)
        side(last, 6)
        z_group(last, 0, P)
        z_group(last, P, TB)
        z_quant(last, 0, P)
        z_quant(last, P, TB)
        project(last, 0)
        project(last, 1, 0, E // 2)
        project(last, 1, E // 2, E)
        o_evac(last, 0, False)
        nc.sync.dma_start(out=o_view(last)[:, 0, :], in_=ores[last][:, 0, :])
        o_evac(last, 1, True, 0, E // 2)
        o_evac(last, 1, True, E // 2, E)
        nc.sync.dma_start(out=o_view(last)[:, 1, :], in_=ores[last][:, 1, :])
